import numpy as np
import ml_dtypes


def mxq(x, axis, fmt="e4m3"):
    dtype, down = {"e4m3": (ml_dtypes.float8_e4m3fn, 7), "e5m2": (ml_dtypes.float8_e5m2, 14)}[fmt]
    v = np.moveaxis(np.asarray(x, np.float32).astype(ml_dtypes.bfloat16).astype(np.float64), axis, -1)
    blocks = v.reshape(v.shape[:-1] + (-1, 32))
    amax = np.abs(blocks).max(-1, keepdims=True)
    byte = np.maximum(np.where(amax > 0, np.frexp(amax)[1] - 1 + 127, 0) - down, 1)
    scale = np.exp2(byte - 127.0)
    codes = (blocks / scale).astype(np.float32).astype(dtype).astype(np.float64)
    return np.moveaxis((codes * scale).reshape(v.shape), -1, axis)


WIDE = False


def mx_kscale(k):
    if not WIDE:
        return np.ones(k)
    levels = np.array([10, -10, 5, -5, 0])
    if k % 512:
        return np.exp2(np.random.permutation(np.resize(levels, k // 32))).repeat(32)
    a = np.empty((k // 512, 16))
    for p in range(k // 512):
        a[p, :8] = np.random.permutation(np.resize(levels, 8))
        for g in range(8):
            far = levels[np.abs(levels - a[p, g]) >= 10]
            a[p, g + 8] = far[np.random.randint(len(far))]
    return np.exp2(a.ravel()).repeat(32)


def f64(x):
    return np.asarray(x).astype(np.float64)


def striped8(idx):
    return np.asarray(idx).reshape(8, -1, 16).transpose(0, 2, 1).reshape(128, -1).astype(np.uint16)


def unstriped8(offs):
    return offs.reshape(8, 16, -1).transpose(0, 2, 1).reshape(8, -1).astype(np.int64)


def pick8(x, idx, run):
    r = np.arange(len(x))
    return x[r[:, None], idx[r % (8 * run) // run]]


E2M1 = np.array([0.0, 0.5, 1.0, 1.5, 2.0, 3.0, 4.0, 6.0, -0.0, -0.5, -1.0, -1.5, -2.0, -3.0, -4.0, -6.0])


def pack_weight(w, fmt):
    k, n = w.shape
    w = f64(np.asarray(w, np.float32).astype(ml_dtypes.bfloat16)).reshape(k // 32, 32, n)
    amax = np.abs(w).max(1)
    if fmt == "e4m3":
        byte = np.frexp(amax)[1] - 1 + 127 - 7
    else:
        mant, ex = np.frexp(amax / 6.0)
        byte = np.where(mant > 0.5, ex, ex - 1) + 127
    byte = np.clip(np.where(amax > 0, byte, 1), 1, 254)
    scaled = (w * np.exp2(127.0 - byte)[:, None, :]).reshape(k, n).astype(np.float32)
    by_word = np.ascontiguousarray(scaled.reshape(k // 512, 128, 4, n).transpose(0, 1, 3, 2))
    if fmt == "e4m3":
        words = by_word.astype(ml_dtypes.float8_e4m3fn).view(np.uint8)
    else:
        c = by_word.astype(ml_dtypes.float4_e2m1fn).view(np.uint8) & 0xF
        words = (c[..., 0::2] | (c[..., 1::2] << 4)).reshape(k // 512, 128, 2 * n)
    return np.ascontiguousarray(words), np.ascontiguousarray(byte.astype(np.uint8).reshape(k // 512, 16, n))


def unpack_weight(words, scales, fmt):
    g, _, n = scales.shape
    words = np.ascontiguousarray(words).reshape(g, 128, n, -1)
    if fmt == "e4m3":
        vals = words.view(ml_dtypes.float8_e4m3fn).astype(np.float64)
    else:
        nib = np.empty((g, 128, n, 4), np.uint8)
        nib[..., 0::2] = words & 0xF
        nib[..., 1::2] = words >> 4
        vals = E2M1[nib]
    vals = vals * np.repeat(np.exp2(scales.astype(np.float64) - 127.0), 8, axis=1)[..., None]
    return vals.transpose(0, 1, 3, 2).reshape(g * 512, n)


D, T, U, X, I, Q = 512, 1024, 1024, 1024, 512, 128


def setup_inputs():
    n = np.random.standard_normal
    idx = np.stack([np.random.permutation(T)[:I] for _ in range(8)])
    idx2 = np.stack([np.random.permutation(U)[:I] for _ in range(8)])
    idx3 = np.stack([np.random.permutation(U)[:I] for _ in range(8)])
    idx4 = np.stack([np.random.permutation(X)[:I] for _ in range(8)])
    idx5 = np.stack([np.random.permutation(X)[:I] for _ in range(8)])
    idx6 = np.stack([np.random.permutation(T)[:I] for _ in range(8)])
    fd = mx_kscale(D)
    cachep = pack_weight(n((D, T)) / fd[:, None], "e4m3")
    draftp = pack_weight(n((D, U)) / fd[:, None], "e2m1")
    archp = pack_weight(n((D, X)) / fd[:, None], "e4m3")
    return {
        "query": (n((D, Q)) * 1.0 / np.sqrt(D) * fd[:, None]).astype(np.float32),
        "cache_words": cachep[0],
        "cache_scales": cachep[1],
        "draft_words": draftp[0],
        "draft_scales": draftp[1],
        "arch_words": archp[0],
        "arch_scales": archp[1],
        "offs": striped8(idx),
        "offs2": striped8(idx2),
        "offs3": striped8(idx3),
        "offs4": striped8(idx4),
        "offs5": striped8(idx5),
        "offs6": striped8(idx6),
    }


def reference(query, cache_words, cache_scales, draft_words, draft_scales, arch_words, arch_scales, offs, offs2, offs3, offs4, offs5, offs6):
    idx = unstriped8(offs)
    idx2 = unstriped8(offs2)
    idx3 = unstriped8(offs3)
    idx4 = unstriped8(offs4)
    idx5 = unstriped8(offs5)
    idx6 = unstriped8(offs6)
    cacheu = unpack_weight(cache_words, cache_scales, "e4m3")
    draftu = unpack_weight(draft_words, draft_scales, "e2m1")
    archu = unpack_weight(arch_words, arch_scales, "e4m3")
    queryq = mxq(f64(query), 0, "e4m3")
    a = queryq.T @ cacheu
    b = queryq.T @ draftu
    c0 = queryq.T @ archu
    f1 = np.zeros((Q, U))
    f1[np.arange(Q)[:, None], idx2[np.arange(Q) % 128 // 16]] = pick8(a, idx, 16)
    f2 = np.zeros((Q, X))
    f2[np.arange(Q)[:, None], idx4[np.arange(Q) % 128 // 16]] = pick8(b, idx3, 16)
    f3 = np.zeros((Q, T))
    f3[np.arange(Q)[:, None], idx6[np.arange(Q) % 128 // 16]] = pick8(c0, idx5, 16)
    aa = a + f3
    bb = b - f1
    cc = np.maximum(c0, f2)
    v = np.maximum(pick8(aa, idx, 16), pick8(bb, idx3, 16))
    y = v - pick8(cc, idx5, 16)
    return y

@@ -1,0 +1,152 @@
+from contextlib import ExitStack
+
+import concourse.mybir as mybir
+
+F32 = mybir.dt.float32
+BF16 = mybir.dt.bfloat16
+I32 = mybir.dt.int32
+U32 = mybir.dt.uint32
+U16 = mybir.dt.uint16
+U8 = mybir.dt.uint8
+FP8X4 = mybir.dt.float8_e4m3fn_x4
+FP4X4 = mybir.dt.float4_e2m1fn_x4
+ALU = mybir.AluOpType
+COPY = mybir.ActivationFunctionType.Copy
+
+P = 128
+PACK = 4
+TOKENS = 1024
+SLOTS = 512
+HALF = SLOTS // 2
+LIST_COLS = SLOTS // 16
+BANK = 512
+FLOPS = 2 * 512 * 128 * 3 * TOKENS
+
+
+def tile_attend_threecorners_three_kernel(
+    tc, query, cache_words, cache_scales, draft_words, draft_scales, arch_words, arch_scales,
+    offs, offs2, offs3, offs4, offs5, offs6, out,
+):
+    nc = tc.nc
+    with ExitStack() as ctx:
+        sb = ctx.enter_context(tc.tile_pool(name="sb", bufs=1))
+        ps = ctx.enter_context(tc.psum_pool(name="ps", bufs=1))
+
+        def scale_plane(name):
+            plane = sb.tile([P, TOKENS], U8, name=name, align_bytes=64)
+            nc.vector.memset(plane[:].bitcast(I32), 0)
+            return plane
+
+        def load_scales(plane, scales):
+            for quad in range(4):
+                nc.sync.dma_start(
+                    out=plane[32 * quad : 32 * quad + 4, :].bitcast(I32),
+                    in_=scales[0, 4 * quad : 4 * quad + 4, :].bitcast(I32),
+                )
+
+        def load_words(name, rows):
+            words = sb.tile([P, rows.shape[1]], U8, name=name, align_bytes=64)
+            nc.sync.dma_start(out=words[:].bitcast(I32), in_=rows.bitcast(I32))
+            return words
+
+        def load_list(name, source):
+            tile = sb.tile([P, LIST_COLS], U16, name=name)
+            nc.sync.dma_start(tile[:], source)
+            return tile
+
+        def zeros(name):
+            tile = sb.tile([P, TOKENS], F32, name=name)
+            nc.vector.memset(tile[:], 0.0)
+            return tile
+
+        def half_list(tile, h):
+            return tile[:, h * LIST_COLS // 2 : (h + 1) * LIST_COLS // 2]
+
+        def half(tile, h):
+            return tile[:, h * HALF : (h + 1) * HALF]
+
+        cache_plane = scale_plane("cache_plane")
+        arch_plane = scale_plane("arch_plane")
+        draft_plane = scale_plane("draft_plane")
+        f1 = zeros("f1")
+        f3 = zeros("f3")
+        f2 = zeros("f2")
+
+        q_raw = sb.tile([P, PACK, P], F32, name="q_raw")
+        nc.sync.dma_start(out=q_raw[:], in_=query.rearrange("(p t) q -> p t q", t=PACK))
+        cache_codes = load_words("cache_codes", cache_words[0].rearrange("p n t -> p (n t)"))
+        load_scales(cache_plane, cache_scales)
+        idx = load_list("idx", offs)
+        idx2 = load_list("idx2", offs2)
+        arch_codes = load_words("arch_codes", arch_words[0].rearrange("p n t -> p (n t)"))
+        load_scales(arch_plane, arch_scales)
+        idx5 = load_list("idx5", offs5)
+        idx6 = load_list("idx6", offs6)
+        draft_codes = load_words("draft_codes", draft_words[0])
+        load_scales(draft_plane, draft_scales)
+        idx3 = load_list("idx3", offs3)
+        idx4 = load_list("idx4", offs4)
+
+        q_bf = sb.tile([P, P, PACK], BF16, name="q_bf", align_bytes=64)
+        nc.vector.tensor_copy(out=q_bf[:], in_=q_raw[:].rearrange("p t q -> p q t"))
+        q_codes = sb.tile([P, P], U32, name="q_codes", align_bytes=64)
+        q_plane = sb.tile([P, P], U8, name="q_plane", align_bytes=64)
+        nc.vector.quantize_mx(
+            out=q_codes[:].bitcast(FP8X4), scales=q_plane[:], in_=q_bf[:].rearrange("p q t -> p (q t)")
+        )
+
+        def scores(name, codes, plane, dtype, copiers):
+            word = codes.shape[1] // TOKENS
+            tile = sb.tile([P, TOKENS], F32, name=name)
+            for j, copier in enumerate(copiers):
+                bank = ps.tile([P, BANK], F32, name="%s_bank%d" % (name, j))
+                nc.tensor.matmul_mx(
+                    out=bank[:],
+                    lhsT=q_codes[:].bitcast(FP8X4),
+                    lhsT_scale=q_plane[:],
+                    rhs=codes[:, word * j * BANK : word * (j + 1) * BANK].bitcast(dtype),
+                    rhs_scale=plane[:, j * BANK : (j + 1) * BANK],
+                    start=True,
+                    stop=True,
+                )
+                copier(out=tile[:, j * BANK : (j + 1) * BANK], in_=bank[:])
+            return tile
+
+        def pass_on(name, source, picked_by, target, placed_by):
+            picked = sb.tile([P, SLOTS], F32, name=name)
+            for h in range(2):
+                nc.vector.tensor_copy(half(picked, h), source[:].indirect(half_list(picked_by, h)))
+                nc.scalar.activation(target[:].indirect(half_list(placed_by, h)), half(picked, h), COPY)
+
+        def look_up(name, source, picked_by):
+            picked = sb.tile([P, SLOTS], F32, name=name)
+            nc.vector.tensor_copy(picked[:], source[:].indirect(picked_by[:]))
+            return picked
+
+        def combine(name, x, y, op, width):
+            tile = sb.tile([P, width], F32, name=name)
+            nc.vector.tensor_tensor(tile[:], x[:], y[:], op)
+            return tile
+
+        on_vector = nc.vector.tensor_copy
+        a = scores("a", cache_codes, cache_plane, FP8X4, (on_vector, nc.scalar.copy))
+        pass_on("a_picked", a, idx, f1, idx2)
+        c0 = scores("c0", arch_codes, arch_plane, FP8X4, (on_vector, on_vector))
+        pass_on("c0_picked", c0, idx5, f3, idx6)
+        b = scores("b", draft_codes, draft_plane, FP4X4, (on_vector, on_vector))
+        pass_on("b_picked", b, idx3, f2, idx4)
+
+        bb = combine("bb", b, f1, ALU.subtract, TOKENS)
+        bb_picked = look_up("bb_picked", bb, idx3)
+        aa = combine("aa", a, f3, ALU.add, TOKENS)
+        aa_picked = look_up("aa_picked", aa, idx)
+        v = combine("v", aa_picked, bb_picked, ALU.max, SLOTS)
+        cc = combine("cc", c0, f2, ALU.max, TOKENS)
+
+        cc_picked = sb.tile([P, SLOTS], F32, name="cc_picked")
+        result = sb.tile([P, SLOTS], F32, name="result")
+        nc.vector.tensor_copy(half(cc_picked, 0), cc[:].indirect(half_list(idx5, 0)))
+        nc.scalar.activation(half(cc_picked, 1), cc[:].indirect(half_list(idx5, 1)), COPY)
+        for h in range(2):
+            nc.vector.tensor_tensor(half(result, h), half(v, h), half(cc_picked, h), ALU.subtract)
+            nc.sync.dma_start(out=out[:, h * HALF : (h + 1) * HALF], in_=half(result, h))

@@ -19,7 +19,6 @@ TOKENS = 1024
 SLOTS = 512
 HALF = SLOTS // 2
 LIST_COLS = SLOTS // 16
-BANK = 512
 FLOPS = 2 * 512 * 128 * 3 * TOKENS
 
 
@@ -32,9 +31,9 @@ def tile_attend_threecorners_three_kernel(
         sb = ctx.enter_context(tc.tile_pool(name="sb", bufs=1))
         ps = ctx.enter_context(tc.psum_pool(name="ps", bufs=1))
 
-        def scale_plane(name):
+        def scale_plane(name, engine):
             plane = sb.tile([P, TOKENS], U8, name=name, align_bytes=64)
-            nc.vector.memset(plane[:].bitcast(I32), 0)
+            engine.memset(plane[:].bitcast(I32), 0)
             return plane
 
         def load_scales(plane, scales):
@@ -43,6 +42,15 @@ def tile_attend_threecorners_three_kernel(
                     out=plane[32 * quad : 32 * quad + 4, :].bitcast(I32),
                     in_=scales[0, 4 * quad : 4 * quad + 4, :].bitcast(I32),
                 )
+
+        def load_scale_rows(name, scales):
+            rows = sb.tile([4, 4, TOKENS // 4], I32, name=name)
+            nc.sync.dma_start(out=rows[:], in_=scales[0].bitcast(I32).rearrange("(quad r) c -> r quad c", r=4))
+            return rows
+
+        def spread_scale_rows(plane, rows):
+            for quad in range(4):
+                nc.vector.tensor_copy(out=plane[32 * quad : 32 * quad + 4, :].bitcast(I32), in_=rows[:, quad, :])
 
         def load_words(name, rows):
             words = sb.tile([P, rows.shape[1]], U8, name=name, align_bytes=64)
@@ -54,9 +62,9 @@ def tile_attend_threecorners_three_kernel(
             nc.sync.dma_start(tile[:], source)
             return tile
 
-        def zeros(name):
+        def zeros(name, engine):
             tile = sb.tile([P, TOKENS], F32, name=name)
-            nc.vector.memset(tile[:], 0.0)
+            engine.memset(tile[:], 0.0)
             return tile
 
         def half_list(tile, h):
@@ -65,83 +73,89 @@ def tile_attend_threecorners_three_kernel(
         def half(tile, h):
             return tile[:, h * HALF : (h + 1) * HALF]
 
-        cache_plane = scale_plane("cache_plane")
-        arch_plane = scale_plane("arch_plane")
-        draft_plane = scale_plane("draft_plane")
-        f1 = zeros("f1")
-        f3 = zeros("f3")
-        f2 = zeros("f2")
+        cache_plane = scale_plane("cache_plane", nc.vector)
+        arch_plane = scale_plane("arch_plane", nc.vector)
+        draft_plane = scale_plane("draft_plane", nc.gpsimd)
+        f1 = zeros("f1", nc.vector)
+        f3 = zeros("f3", nc.gpsimd)
+        f2 = zeros("f2", nc.gpsimd)
 
+        cache_rows = load_scale_rows("cache_rows", cache_scales)
         q_raw = sb.tile([P, PACK, P], F32, name="q_raw")
         nc.sync.dma_start(out=q_raw[:], in_=query.rearrange("(p t) q -> p t q", t=PACK))
         cache_codes = load_words("cache_codes", cache_words[0].rearrange("p n t -> p (n t)"))
-        load_scales(cache_plane, cache_scales)
+        arch_rows = load_scale_rows("arch_rows", arch_scales)
+        arch_codes = load_words("arch_codes", arch_words[0].rearrange("p n t -> p (n t)"))
         idx = load_list("idx", offs)
         idx2 = load_list("idx2", offs2)
-        arch_codes = load_words("arch_codes", arch_words[0].rearrange("p n t -> p (n t)"))
-        load_scales(arch_plane, arch_scales)
-        idx5 = load_list("idx5", offs5)
-        idx6 = load_list("idx6", offs6)
         draft_codes = load_words("draft_codes", draft_words[0])
+        idx5 = load_list("idx5", offs5)
         load_scales(draft_plane, draft_scales)
         idx3 = load_list("idx3", offs3)
+        idx6 = load_list("idx6", offs6)
         idx4 = load_list("idx4", offs4)
 
+        spread_scale_rows(cache_plane, cache_rows)
         q_bf = sb.tile([P, P, PACK], BF16, name="q_bf", align_bytes=64)
-        nc.vector.tensor_copy(out=q_bf[:], in_=q_raw[:].rearrange("p t q -> p q t"))
+        q_dealt = q_raw[:].rearrange("p t q -> p q t")
+        nc.vector.tensor_copy(out=q_bf[:, : P // 2, :], in_=q_dealt[:, : P // 2, :])
+        nc.scalar.copy(out=q_bf[:, P // 2 :, :], in_=q_dealt[:, P // 2 :, :])
         q_codes = sb.tile([P, P], U32, name="q_codes", align_bytes=64)
         q_plane = sb.tile([P, P], U8, name="q_plane", align_bytes=64)
         nc.vector.quantize_mx(
             out=q_codes[:].bitcast(FP8X4), scales=q_plane[:], in_=q_bf[:].rearrange("p q t -> p (q t)")
         )
 
+        spread_scale_rows(arch_plane, arch_rows)
+
         def scores(name, codes, plane, dtype, copiers):
             word = codes.shape[1] // TOKENS
-            tile = sb.tile([P, TOKENS], F32, name=name)
+            tile = sb.tile([P, TOKENS], F32, name=name, tag=name)
+            width = TOKENS // len(copiers)
             for j, copier in enumerate(copiers):
-                bank = ps.tile([P, BANK], F32, name="%s_bank%d" % (name, j))
+                bank = ps.tile([P, width], F32, name="%s_bank%d" % (name, j))
                 nc.tensor.matmul_mx(
                     out=bank[:],
                     lhsT=q_codes[:].bitcast(FP8X4),
                     lhsT_scale=q_plane[:],
-                    rhs=codes[:, word * j * BANK : word * (j + 1) * BANK].bitcast(dtype),
-                    rhs_scale=plane[:, j * BANK : (j + 1) * BANK],
+                    rhs=codes[:, word * j * width : word * (j + 1) * width].bitcast(dtype),
+                    rhs_scale=plane[:, j * width : (j + 1) * width],
                     start=True,
                     stop=True,
                 )
-                copier(out=tile[:, j * BANK : (j + 1) * BANK], in_=bank[:])
+                copier(out=tile[:, j * width : (j + 1) * width], in_=bank[:])
             return tile
 
-        def pass_on(name, source, picked_by, target, placed_by):
+        def pass_on(name, source, picked_by, target, placed_by, pieces):
             picked = sb.tile([P, SLOTS], F32, name=name)
-            for h in range(2):
-                nc.vector.tensor_copy(half(picked, h), source[:].indirect(half_list(picked_by, h)))
-                nc.scalar.activation(target[:].indirect(half_list(placed_by, h)), half(picked, h), COPY)
+            for j in range(pieces):
+                slots = slice(j * SLOTS // pieces, (j + 1) * SLOTS // pieces)
+                entries = slice(j * LIST_COLS // pieces, (j + 1) * LIST_COLS // pieces)
+                nc.vector.tensor_copy(picked[:, slots], source[:].indirect(picked_by[:, entries]))
+                nc.scalar.activation(target[:].indirect(placed_by[:, entries]), picked[:, slots], COPY)
 
-        def look_up(name, source, picked_by):
-            picked = sb.tile([P, SLOTS], F32, name=name)
-            nc.vector.tensor_copy(picked[:], source[:].indirect(picked_by[:]))
-            return picked
-
-        def combine(name, x, y, op, width):
-            tile = sb.tile([P, width], F32, name=name)
-            nc.vector.tensor_tensor(tile[:], x[:], y[:], op)
-            return tile
-
-        on_vector = nc.vector.tensor_copy
-        a = scores("a", cache_codes, cache_plane, FP8X4, (on_vector, nc.scalar.copy))
-        pass_on("a_picked", a, idx, f1, idx2)
-        c0 = scores("c0", arch_codes, arch_plane, FP8X4, (on_vector, on_vector))
-        pass_on("c0_picked", c0, idx5, f3, idx6)
+        on_vector, on_scalar = nc.vector.tensor_copy, nc.scalar.copy
+        a = scores("a", cache_codes, cache_plane, FP8X4, (on_scalar, on_vector, on_scalar, on_vector))
+        c0 = scores("c0", arch_codes, arch_plane, FP8X4, (on_scalar, on_scalar))
+        pass_on("a_picked", a, idx, f1, idx2, 1)
+        pass_on("c0_picked", c0, idx5, f3, idx6, 1)
         b = scores("b", draft_codes, draft_plane, FP4X4, (on_vector, on_vector))
-        pass_on("b_picked", b, idx3, f2, idx4)
+        pass_on("b_picked", b, idx3, f2, idx4, 1)
 
-        bb = combine("bb", b, f1, ALU.subtract, TOKENS)
-        bb_picked = look_up("bb_picked", bb, idx3)
-        aa = combine("aa", a, f3, ALU.add, TOKENS)
-        aa_picked = look_up("aa_picked", aa, idx)
-        v = combine("v", aa_picked, bb_picked, ALU.max, SLOTS)
-        cc = combine("cc", c0, f2, ALU.max, TOKENS)
+        bb = sb.tile([P, TOKENS], F32, name="bb")
+        nc.vector.tensor_tensor(bb[:], b[:], f1[:], ALU.subtract)
+        bb_picked = sb.tile([P, SLOTS], F32, name="bb_picked")
+        nc.vector.tensor_copy(bb_picked[:], bb[:].indirect(idx3[:]))
+        aa = sb.tile([P, TOKENS], F32, name="aa", tag="b")
+        nc.vector.tensor_tensor(aa[:], a[:], f3[:], ALU.add)
+        aa_picked = sb.tile([P, SLOTS], F32, name="aa_picked")
+        v = sb.tile([P, SLOTS], F32, name="v")
+        for h in range(2):
+            nc.vector.tensor_copy(half(aa_picked, h), aa[:].indirect(half_list(idx, h)))
+        for h in range(2):
+            nc.vector.tensor_tensor(half(v, h), half(aa_picked, h), half(bb_picked, h), ALU.max)
+        cc = sb.tile([P, TOKENS], F32, name="cc", tag="b")
+        nc.vector.tensor_tensor(cc[:], c0[:], f2[:], ALU.max)
 
         cc_picked = sb.tile([P, SLOTS], F32, name="cc_picked")
         result = sb.tile([P, SLOTS], F32, name="result")

@@ -43,27 +43,20 @@ def tile_attend_threecorners_three_kernel(
                     in_=scales[0, 4 * quad : 4 * quad + 4, :].bitcast(I32),
                 )
 
-        def load_scale_rows(name, scales):
-            rows = sb.tile([4, 4, TOKENS // 4], I32, name=name)
-            nc.sync.dma_start(out=rows[:], in_=scales[0].bitcast(I32).rearrange("(quad r) c -> r quad c", r=4))
-            return rows
+        def words_tile(name, rows):
+            return sb.tile([P, rows.shape[1]], U8, name=name, tag=name, align_bytes=64)
 
-        def spread_scale_rows(plane, rows):
-            for quad in range(4):
-                nc.vector.tensor_copy(out=plane[32 * quad : 32 * quad + 4, :].bitcast(I32), in_=rows[:, quad, :])
-
-        def load_words(name, rows):
-            words = sb.tile([P, rows.shape[1]], U8, name=name, align_bytes=64)
-            nc.sync.dma_start(out=words[:].bitcast(I32), in_=rows.bitcast(I32))
-            return words
+        def load_words(words, rows, first, last):
+            cols = slice(first * rows.shape[1] // TOKENS, last * rows.shape[1] // TOKENS)
+            nc.sync.dma_start(out=words[:, cols].bitcast(I32), in_=rows[:, cols].bitcast(I32))
 
         def load_list(name, source):
             tile = sb.tile([P, LIST_COLS], U16, name=name)
             nc.sync.dma_start(tile[:], source)
             return tile
 
-        def zeros(name, engine):
-            tile = sb.tile([P, TOKENS], F32, name=name)
+        def zeros(name, engine, tag):
+            tile = sb.tile([P, TOKENS], F32, name=name, tag=tag, align_bytes=64)
             engine.memset(tile[:], 0.0)
             return tile
 
@@ -73,30 +66,35 @@ def tile_attend_threecorners_three_kernel(
         def half(tile, h):
             return tile[:, h * HALF : (h + 1) * HALF]
 
-        cache_plane = scale_plane("cache_plane", nc.vector)
+        cache_plane = scale_plane("cache_plane", nc.gpsimd)
         arch_plane = scale_plane("arch_plane", nc.vector)
-        draft_plane = scale_plane("draft_plane", nc.gpsimd)
-        f1 = zeros("f1", nc.vector)
-        f3 = zeros("f3", nc.gpsimd)
-        f2 = zeros("f2", nc.gpsimd)
+        draft_plane = scale_plane("draft_plane", nc.vector)
+        f1 = zeros("f1", nc.vector, "f1")
+        f3 = zeros("f3", nc.vector, "f3")
 
-        cache_rows = load_scale_rows("cache_rows", cache_scales)
         q_raw = sb.tile([P, PACK, P], F32, name="q_raw")
         nc.sync.dma_start(out=q_raw[:], in_=query.rearrange("(p t) q -> p t q", t=PACK))
-        cache_codes = load_words("cache_codes", cache_words[0].rearrange("p n t -> p (n t)"))
-        arch_rows = load_scale_rows("arch_rows", arch_scales)
-        arch_codes = load_words("arch_codes", arch_words[0].rearrange("p n t -> p (n t)"))
+        cache_rows = cache_words[0].rearrange("p n t -> p (n t)")
+        arch_rows = arch_words[0].rearrange("p n t -> p (n t)")
+        cache_codes = words_tile("cache_codes", cache_rows)
+        arch_codes = words_tile("arch_codes", arch_rows)
+        draft_codes = words_tile("draft_codes", draft_words[0])
+        load_scales(cache_plane, cache_scales)
+        load_words(cache_codes, cache_rows, 0, TOKENS // 2)
+        load_words(cache_codes, cache_rows, TOKENS // 2, TOKENS)
+        load_words(arch_codes, arch_rows, 0, TOKENS // 2)
         idx = load_list("idx", offs)
+        load_scales(arch_plane, arch_scales)
+        load_words(arch_codes, arch_rows, TOKENS // 2, TOKENS)
         idx2 = load_list("idx2", offs2)
-        draft_codes = load_words("draft_codes", draft_words[0])
         idx5 = load_list("idx5", offs5)
-        load_scales(draft_plane, draft_scales)
+        load_words(draft_codes, draft_words[0], 0, TOKENS)
         idx3 = load_list("idx3", offs3)
+        load_scales(draft_plane, draft_scales)
         idx6 = load_list("idx6", offs6)
         idx4 = load_list("idx4", offs4)
 
-        spread_scale_rows(cache_plane, cache_rows)
-        q_bf = sb.tile([P, P, PACK], BF16, name="q_bf", align_bytes=64)
+        q_bf = sb.tile([P, P, PACK], BF16, name="q_bf", tag="q_bf", align_bytes=64)
         q_dealt = q_raw[:].rearrange("p t q -> p q t")
         nc.vector.tensor_copy(out=q_bf[:, : P // 2, :], in_=q_dealt[:, : P // 2, :])
         nc.scalar.copy(out=q_bf[:, P // 2 :, :], in_=q_dealt[:, P // 2 :, :])
@@ -106,7 +104,7 @@ def tile_attend_threecorners_three_kernel(
             out=q_codes[:].bitcast(FP8X4), scales=q_plane[:], in_=q_bf[:].rearrange("p q t -> p (q t)")
         )
 
-        spread_scale_rows(arch_plane, arch_rows)
+        f2 = zeros("f2", nc.vector, "q_bf")
 
         def scores(name, codes, plane, dtype, copiers):
             word = codes.shape[1] // TOKENS
@@ -136,7 +134,7 @@ def tile_attend_threecorners_three_kernel(
 
         on_vector, on_scalar = nc.vector.tensor_copy, nc.scalar.copy
         a = scores("a", cache_codes, cache_plane, FP8X4, (on_scalar, on_vector, on_scalar, on_vector))
-        c0 = scores("c0", arch_codes, arch_plane, FP8X4, (on_scalar, on_scalar))
+        c0 = scores("c0", arch_codes, arch_plane, FP8X4, (on_scalar, on_vector))
         pass_on("a_picked", a, idx, f1, idx2, 1)
         pass_on("c0_picked", c0, idx5, f3, idx6, 1)
         b = scores("b", draft_codes, draft_plane, FP4X4, (on_vector, on_vector))

@@ -110,6 +110,7 @@ def tile_attend_threecorners_three_kernel(
             word = codes.shape[1] // TOKENS
             tile = sb.tile([P, TOKENS], F32, name=name, tag=name)
             width = TOKENS // len(copiers)
+            banks = []
             for j, copier in enumerate(copiers):
                 bank = ps.tile([P, width], F32, name="%s_bank%d" % (name, j))
                 nc.tensor.matmul_mx(
@@ -122,7 +123,8 @@ def tile_attend_threecorners_three_kernel(
                     stop=True,
                 )
                 copier(out=tile[:, j * width : (j + 1) * width], in_=bank[:])
-            return tile
+                banks.append(bank)
+            return tile, banks
 
         def pass_on(name, source, picked_by, target, placed_by, pieces):
             picked = sb.tile([P, SLOTS], F32, name=name)
@@ -133,15 +135,17 @@ def tile_attend_threecorners_three_kernel(
                 nc.scalar.activation(target[:].indirect(placed_by[:, entries]), picked[:, slots], COPY)
 
         on_vector, on_scalar = nc.vector.tensor_copy, nc.scalar.copy
-        a = scores("a", cache_codes, cache_plane, FP8X4, (on_scalar, on_vector, on_scalar, on_vector))
-        c0 = scores("c0", arch_codes, arch_plane, FP8X4, (on_scalar, on_vector))
-        pass_on("a_picked", a, idx, f1, idx2, 1)
+        a, a_banks = scores("a", cache_codes, cache_plane, FP8X4, (on_scalar, on_vector, on_scalar, on_vector))
+        c0, c0_banks = scores("c0", arch_codes, arch_plane, FP8X4, (on_scalar, on_vector))
+        pass_on("a_picked", a, idx, f1, idx2, 2)
         pass_on("c0_picked", c0, idx5, f3, idx6, 1)
-        b = scores("b", draft_codes, draft_plane, FP4X4, (on_vector, on_vector))
+        b, b_banks = scores("b", draft_codes, draft_plane, FP4X4, (on_vector, on_vector))
         pass_on("b_picked", b, idx3, f2, idx4, 1)
 
         bb = sb.tile([P, TOKENS], F32, name="bb")
-        nc.vector.tensor_tensor(bb[:], b[:], f1[:], ALU.subtract)
+        mid = TOKENS // 2
+        nc.gpsimd.tensor_tensor(bb[:, :mid], b[:, :mid], f1[:, :mid], ALU.subtract)
+        nc.vector.tensor_tensor(bb[:, mid:], b_banks[1][:], f1[:, mid:], ALU.subtract)
         bb_picked = sb.tile([P, SLOTS], F32, name="bb_picked")
         nc.vector.tensor_copy(bb_picked[:], bb[:].indirect(idx3[:]))
         aa = sb.tile([P, TOKENS], F32, name="aa", tag="b")

from contextlib import ExitStack

import concourse.mybir as mybir

F32 = mybir.dt.float32
BF16 = mybir.dt.bfloat16
I32 = mybir.dt.int32
U32 = mybir.dt.uint32
U16 = mybir.dt.uint16
U8 = mybir.dt.uint8
FP8X4 = mybir.dt.float8_e4m3fn_x4
FP4X4 = mybir.dt.float4_e2m1fn_x4
ALU = mybir.AluOpType
COPY = mybir.ActivationFunctionType.Copy

P = 128
PACK = 4
TOKENS = 1024
SLOTS = 512
HALF = SLOTS // 2
LIST_COLS = SLOTS // 16
FLOPS = 2 * 512 * 128 * 3 * TOKENS


def tile_attend_threecorners_three_kernel(
    tc, query, cache_words, cache_scales, draft_words, draft_scales, arch_words, arch_scales,
    offs, offs2, offs3, offs4, offs5, offs6, out,
):
    nc = tc.nc
    with ExitStack() as ctx:
        sb = ctx.enter_context(tc.tile_pool(name="sb", bufs=1))
        ps = ctx.enter_context(tc.psum_pool(name="ps", bufs=1))

        def scale_plane(name, engine):
            plane = sb.tile([P, TOKENS], U8, name=name, align_bytes=64)
            engine.memset(plane[:].bitcast(I32), 0)
            return plane

        def load_scales(plane, scales):
            for quad in range(4):
                nc.sync.dma_start(
                    out=plane[32 * quad : 32 * quad + 4, :].bitcast(I32),
                    in_=scales[0, 4 * quad : 4 * quad + 4, :].bitcast(I32),
                )

        def words_tile(name, rows):
            return sb.tile([P, rows.shape[1]], U8, name=name, tag=name, align_bytes=64)

        def load_words(words, rows, first, last):
            cols = slice(first * rows.shape[1] // TOKENS, last * rows.shape[1] // TOKENS)
            nc.sync.dma_start(out=words[:, cols].bitcast(I32), in_=rows[:, cols].bitcast(I32))

        def load_list(name, source):
            tile = sb.tile([P, LIST_COLS], U16, name=name)
            nc.sync.dma_start(tile[:], source)
            return tile

        def zeros(name, engine, tag):
            tile = sb.tile([P, TOKENS], F32, name=name, tag=tag, align_bytes=64)
            engine.memset(tile[:], 0.0)
            return tile

        def half_list(tile, h):
            return tile[:, h * LIST_COLS // 2 : (h + 1) * LIST_COLS // 2]

        def half(tile, h):
            return tile[:, h * HALF : (h + 1) * HALF]

        cache_plane = scale_plane("cache_plane", nc.gpsimd)
        arch_plane = scale_plane("arch_plane", nc.vector)
        draft_plane = scale_plane("draft_plane", nc.vector)
        f1 = zeros("f1", nc.vector, "f1")
        f3 = zeros("f3", nc.vector, "f3")

        q_raw = sb.tile([P, PACK, P], F32, name="q_raw")
        nc.sync.dma_start(out=q_raw[:], in_=query.rearrange("(p t) q -> p t q", t=PACK))
        cache_rows = cache_words[0].rearrange("p n t -> p (n t)")
        arch_rows = arch_words[0].rearrange("p n t -> p (n t)")
        cache_codes = words_tile("cache_codes", cache_rows)
        arch_codes = words_tile("arch_codes", arch_rows)
        draft_codes = words_tile("draft_codes", draft_words[0])
        load_scales(cache_plane, cache_scales)
        load_words(cache_codes, cache_rows, 0, TOKENS // 2)
        load_words(cache_codes, cache_rows, TOKENS // 2, TOKENS)
        load_words(arch_codes, arch_rows, 0, TOKENS // 2)
        idx = load_list("idx", offs)
        load_scales(arch_plane, arch_scales)
        load_words(arch_codes, arch_rows, TOKENS // 2, TOKENS)
        idx2 = load_list("idx2", offs2)
        idx5 = load_list("idx5", offs5)
        load_words(draft_codes, draft_words[0], 0, TOKENS)
        idx3 = load_list("idx3", offs3)
        load_scales(draft_plane, draft_scales)
        idx6 = load_list("idx6", offs6)
        idx4 = load_list("idx4", offs4)

        q_bf = sb.tile([P, P, PACK], BF16, name="q_bf", tag="q_bf", align_bytes=64)
        q_dealt = q_raw[:].rearrange("p t q -> p q t")
        nc.vector.tensor_copy(out=q_bf[:, : P // 2, :], in_=q_dealt[:, : P // 2, :])
        nc.scalar.copy(out=q_bf[:, P // 2 :, :], in_=q_dealt[:, P // 2 :, :])
        q_codes = sb.tile([P, P], U32, name="q_codes", align_bytes=64)
        q_plane = sb.tile([P, P], U8, name="q_plane", align_bytes=64)
        nc.vector.quantize_mx(
            out=q_codes[:].bitcast(FP8X4), scales=q_plane[:], in_=q_bf[:].rearrange("p q t -> p (q t)")
        )

        f2 = zeros("f2", nc.vector, "q_bf")

        def scores(name, codes, plane, dtype, copiers):
            word = codes.shape[1] // TOKENS
            tile = sb.tile([P, TOKENS], F32, name=name, tag=name)
            width = TOKENS // len(copiers)
            banks = []
            for j, copier in enumerate(copiers):
                bank = ps.tile([P, width], F32, name="%s_bank%d" % (name, j))
                nc.tensor.matmul_mx(
                    out=bank[:],
                    lhsT=q_codes[:].bitcast(FP8X4),
                    lhsT_scale=q_plane[:],
                    rhs=codes[:, word * j * width : word * (j + 1) * width].bitcast(dtype),
                    rhs_scale=plane[:, j * width : (j + 1) * width],
                    start=True,
                    stop=True,
                )
                copier(out=tile[:, j * width : (j + 1) * width], in_=bank[:])
                banks.append(bank)
            return tile, banks

        def pass_on(name, source, picked_by, target, placed_by, pieces):
            picked = sb.tile([P, SLOTS], F32, name=name)
            for j in range(pieces):
                slots = slice(j * SLOTS // pieces, (j + 1) * SLOTS // pieces)
                entries = slice(j * LIST_COLS // pieces, (j + 1) * LIST_COLS // pieces)
                nc.vector.tensor_copy(picked[:, slots], source[:].indirect(picked_by[:, entries]))
                nc.scalar.activation(target[:].indirect(placed_by[:, entries]), picked[:, slots], COPY)

        on_vector, on_scalar = nc.vector.tensor_copy, nc.scalar.copy
        a, a_banks = scores("a", cache_codes, cache_plane, FP8X4, (on_scalar, on_vector, on_scalar, on_vector))
        c0, c0_banks = scores("c0", arch_codes, arch_plane, FP8X4, (on_scalar, on_vector))
        pass_on("a_picked", a, idx, f1, idx2, 2)
        pass_on("c0_picked", c0, idx5, f3, idx6, 1)
        b, b_banks = scores("b", draft_codes, draft_plane, FP4X4, (on_vector, on_vector))
        pass_on("b_picked", b, idx3, f2, idx4, 1)

        bb = sb.tile([P, TOKENS], F32, name="bb")
        mid = TOKENS // 2
        nc.gpsimd.tensor_tensor(bb[:, :mid], b[:, :mid], f1[:, :mid], ALU.subtract)
        nc.vector.tensor_tensor(bb[:, mid:], b_banks[1][:], f1[:, mid:], ALU.subtract)
        bb_picked = sb.tile([P, SLOTS], F32, name="bb_picked")
        nc.vector.tensor_copy(bb_picked[:], bb[:].indirect(idx3[:]))
        aa = sb.tile([P, TOKENS], F32, name="aa", tag="b")
        nc.vector.tensor_tensor(aa[:], a[:], f3[:], ALU.add)
        aa_picked = sb.tile([P, SLOTS], F32, name="aa_picked")
        v = sb.tile([P, SLOTS], F32, name="v")
        for h in range(2):
            nc.vector.tensor_copy(half(aa_picked, h), aa[:].indirect(half_list(idx, h)))
        for h in range(2):
            nc.vector.tensor_tensor(half(v, h), half(aa_picked, h), half(bb_picked, h), ALU.max)
        cc = sb.tile([P, TOKENS], F32, name="cc", tag="b")
        nc.vector.tensor_tensor(cc[:], c0[:], f2[:], ALU.max)

        cc_picked = sb.tile([P, SLOTS], F32, name="cc_picked")
        result = sb.tile([P, SLOTS], F32, name="result")
        nc.vector.tensor_copy(half(cc_picked, 0), cc[:].indirect(half_list(idx5, 0)))
        nc.scalar.activation(half(cc_picked, 1), cc[:].indirect(half_list(idx5, 1)), COPY)
        for h in range(2):
            nc.vector.tensor_tensor(half(result, h), half(v, h), half(cc_picked, h), ALU.subtract)
            nc.sync.dma_start(out=out[:, h * HALF : (h + 1) * HALF], in_=half(result, h))
